import numpy as np
import ml_dtypes


def mxq(x, axis, fmt="e4m3"):
    dtype, down = {"e4m3": (ml_dtypes.float8_e4m3fn, 7), "e5m2": (ml_dtypes.float8_e5m2, 14)}[fmt]
    v = np.moveaxis(np.asarray(x, np.float32).astype(ml_dtypes.bfloat16).astype(np.float64), axis, -1)
    blocks = v.reshape(v.shape[:-1] + (-1, 32))
    amax = np.abs(blocks).max(-1, keepdims=True)
    byte = np.maximum(np.where(amax > 0, np.frexp(amax)[1] - 1 + 127, 0) - down, 1)
    scale = np.exp2(byte - 127.0)
    codes = (blocks / scale).astype(np.float32).astype(dtype).astype(np.float64)
    return np.moveaxis((codes * scale).reshape(v.shape), -1, axis)


WIDE = False


def mx_kscale(k):
    if not WIDE:
        return np.ones(k)
    levels = np.array([10, -10, 5, -5, 0])
    if k % 512:
        return np.exp2(np.random.permutation(np.resize(levels, k // 32))).repeat(32)
    a = np.empty((k // 512, 16))
    for p in range(k // 512):
        a[p, :8] = np.random.permutation(np.resize(levels, 8))
        for g in range(8):
            far = levels[np.abs(levels - a[p, g]) >= 10]
            a[p, g + 8] = far[np.random.randint(len(far))]
    return np.exp2(a.ravel()).repeat(32)


def f64(x):
    return np.asarray(x).astype(np.float64)


def striped(idx):
    return np.tile(idx.reshape(-1, 16).T, (8, 1)).astype(np.uint16)


def unstriped(offs):
    return offs[:16].T.reshape(-1).astype(np.int64)


def striped8(idx):
    return np.concatenate([x.reshape(-1, 16).T for x in idx]).astype(np.uint16)


def runs(offs, k):
    lists = np.stack([offs[16 * r : 16 * r + 16].T.reshape(-1) for r in range(8)]).astype(np.int64)
    return lists[np.arange(k) % 512 // 64]


def pack_weight(w):
    k, n = w.shape
    w = f64(np.asarray(w, np.float32).astype(ml_dtypes.bfloat16)).reshape(k // 32, 32, n)
    amax = np.abs(w).max(1)
    byte = np.clip(np.where(amax > 0, np.frexp(amax)[1] - 1 + 127 - 7, 1), 1, 254)
    scaled = (w * np.exp2(127.0 - byte)[:, None, :]).reshape(k, n).astype(np.float32)
    words = np.ascontiguousarray(scaled.reshape(k // 512, 128, 4, n).transpose(0, 1, 3, 2)).astype(ml_dtypes.float8_e4m3fn).view(np.uint8)
    return words, np.ascontiguousarray(byte.astype(np.uint8).reshape(k // 512, 16, n))


def unpack_weight(words, scales):
    g, p, n, _ = words.shape
    vals = np.ascontiguousarray(words).view(ml_dtypes.float8_e4m3fn).astype(np.float64) * np.repeat(np.exp2(scales.astype(np.float64) - 127.0), 8, axis=1)[..., None]
    return vals.transpose(0, 1, 3, 2).reshape(g * 512, n)


K, T, S, N, H, U = 512, 2048, 512, 512, 512, 1024


def setup_inputs():
    n = np.random.standard_normal
    s = mx_kscale(K)[:, None]
    u = mx_kscale(H)
    packed_xT = pack_weight(n((K, T)) * s)
    return {
        "x_words": packed_xT[0],
        "x_scales": packed_xT[1],
        "w1": (n((K, H)) / np.sqrt(K) / s).astype(np.float32),
        "w2": (n((K, H)) / np.sqrt(K) / s).astype(np.float32),
        "gn": (np.random.uniform(0.5, 1.5, (H, 1)) * u[:, None]).astype(np.float32),
        "w3": (n((H, N)) / np.sqrt(H) / u[:, None]).astype(np.float32),
        "mem": n((N, U)).astype(np.float32),
        "offs": striped(np.random.permutation(T)[:S]),
        "two": striped(np.random.permutation(T)[:S]),
        "n1": striped8(np.stack([np.random.permutation(S) for _ in range(8)])),
        "n2": striped8(np.stack([np.random.permutation(S) for _ in range(8)])),
        "slot": striped8(np.stack([np.random.permutation(U)[:S] for _ in range(8)])),
    }


def reference(x_words, x_scales, w1, w2, gn, w3, mem, offs, two, n1, n2, slot):
    xq = unpack_weight(x_words, x_scales)[:, unstriped(offs)]
    y = mxq(f64(w1), 0, "e4m3").T @ xq
    p = np.maximum(y, y[np.arange(H)[:, None], runs(n1, H)])
    x_two = unpack_weight(x_words, x_scales)[:, unstriped(two)]
    c = mxq(f64(w2), 0, "e4m3").T @ x_two
    qv = np.minimum(c, c[np.arange(H)[:, None], runs(n2, H)])
    z = f64(gn) * (p * (qv[np.arange(H)[:, None], runs(n1, H)]) - (qv * (p[np.arange(H)[:, None], runs(n2, H)])))
    h = mxq(f64(w3), 0, "e4m3").T @ mxq(z, 0, "e4m3")
    out = f64(mem).copy()
    out[np.arange(N)[:, None], runs(slot, N)] = h
    return out

@@ -1,0 +1,251 @@
+from contextlib import ExitStack
+
+import concourse.mybir as mybir
+
+K, T, S, N, H, U = 512, 2048, 512, 512, 512, 1024
+FLOPS = 3 * 2 * 512 * 512 * 512
+
+F32 = mybir.dt.float32
+BF16 = mybir.dt.bfloat16
+I32 = mybir.dt.int32
+U32 = mybir.dt.uint32
+U16 = mybir.dt.uint16
+U8 = mybir.dt.uint8
+FP8X4 = mybir.dt.float8_e4m3fn_x4
+ALU = mybir.AluOpType
+COPY = mybir.ActivationFunctionType.Copy
+
+P = 128
+PACK = 4
+HALF = S // 2
+SLICE = 128
+SLICES = S // SLICE
+
+
+def tile_picked_wedge2_none_p_kernel(
+    tc, x_words, x_scales, w1, w2, gn, w3, mem, offs, two, n1, n2, slot, out
+):
+    nc = tc.nc
+    with ExitStack() as ctx:
+        keep = ctx.enter_context(tc.tile_pool(name="keep", bufs=1))
+        psum = ctx.enter_context(tc.psum_pool(name="psum", bufs=1))
+
+        def sb(name, shape, dtype, tag=None):
+            return keep.tile(shape, dtype, name=name, tag=tag or name, align_bytes=64)
+
+        def load_list(name, src):
+            t = keep.tile([P, S // 16], U16, name=name)
+            nc.sync.dma_start(t[:], src)
+            return t
+
+        def cols(lst, start, count):
+            return lst[:, start // 16 : (start + count) // 16]
+
+        def load_weight(name, w):
+            raw = sb(name + "_raw", [P, PACK, 512], F32)
+            nc.sync.dma_start(raw[:], w.rearrange("(p j) c -> p j c", j=PACK))
+            return raw
+
+        xs = sb("xs", [P, T], U8)
+        nc.vector.memset(xs[:].bitcast(I32), 0)
+        w1_raw = load_weight("w1", w1)
+        for q in range(4):
+            nc.sync.dma_start(xs[32 * q : 32 * q + 4, :].bitcast(I32), x_scales[0, 4 * q : 4 * q + 4, :].bitcast(I32))
+        offs_t = load_list("offs_t", offs)
+        xw = sb("xw", [P, T], U32)
+        nc.sync.dma_start(xw[:].bitcast(I32), x_words[0].rearrange("p n t -> p (n t)").bitcast(I32))
+        two_t = load_list("two_t", two)
+        w2_raw = load_weight("w2", w2)
+        n1_t = load_list("n1_t", n1)
+        n2_t = load_list("n2_t", n2)
+        w3_raw = load_weight("w3", w3)
+        gain = sb("gain", [P, PACK], F32)
+        nc.sync.dma_start(gain[:], gn.rearrange("(p t) o -> p (t o)", t=PACK))
+        slot_t = load_list("slot_t", slot)
+        page = []
+        mem_rows = mem.rearrange("(p t) u -> t p u", t=PACK)
+        out_rows = out.rearrange("(p t) u -> t p u", t=PACK)
+        for t in range(PACK):
+            pg = sb("page%d" % t, [P, U], F32)
+            nc.sync.dma_start(pg[:], mem_rows[t])
+            page.append(pg)
+
+        def cast_weight(name, raw, engines):
+            halves = []
+            for u in range(2):
+                g = sb("%s_bf%d" % (name, u), [P, 2 * P * PACK], BF16)
+                dst = g[:].rearrange("p (t m j) -> p m t j", t=2, j=PACK)
+                src = raw[:].rearrange("p j (m t) -> p m t j", t=PACK)[:, :, 2 * u : 2 * u + 2, :]
+                if engines[u] == "v":
+                    nc.vector.tensor_copy(dst, src)
+                elif engines[u] == "g":
+                    nc.gpsimd.tensor_scalar(dst, src, 1.0, 0.0, ALU.mult, ALU.add)
+                else:
+                    nc.scalar.copy(dst, src)
+                halves.append(g)
+            return halves
+
+        def quantize_weight(name, halves):
+            made = []
+            for u in range(2):
+                codes = sb("%s_codes%d" % (name, u), [P, 2 * P], U32)
+                scales = sb("%s_scales%d" % (name, u), [P, 2 * P], U8)
+                nc.vector.quantize_mx(out=codes[:].bitcast(FP8X4), scales=scales[:], in_=halves[u][:])
+                made.append((codes, scales))
+            return made
+
+        def product(dst, wq, t, codes, scales):
+            wc, ws = wq[t // 2]
+            m = slice((t % 2) * P, (t % 2 + 1) * P)
+            nc.tensor.matmul_mx(
+                out=dst, lhsT=wc[:, m].bitcast(FP8X4), lhsT_scale=ws[:, m],
+                rhs=codes.bitcast(FP8X4), rhs_scale=scales, start=True, stop=True,
+            )
+
+        def gather(engine, dst, window, offsets):
+            if engine == "v":
+                nc.vector.tensor_copy(dst, window[:].indirect(offsets))
+            else:
+                nc.scalar.activation(dst, window[:].indirect(offsets), COPY)
+
+        def evacuate(engine, dst, src):
+            if engine == "v":
+                nc.vector.tensor_copy(dst, src)
+            else:
+                nc.scalar.copy(dst, src)
+
+        s1 = sb("s1", [P, S], U8)
+        nc.vector.tensor_copy(s1[:], xs[:].indirect(offs_t[:]))
+        w1_q = quantize_weight("w1", cast_weight("w1", w1_raw, "vs"))
+        s2 = sb("s2", [P, S], U8)
+        nc.vector.tensor_copy(s2[:], xs[:].indirect(two_t[:]))
+        x1 = sb("x1", [P, S], U32)
+        nc.vector.tensor_copy(x1[:], xw[:].indirect(offs_t[:]))
+        y_ps = []
+        for t in range(PACK):
+            b = psum.tile([P, S], F32, name="y_ps%d" % t, tag="bank%d" % t)
+            product(b[:], w1_q, t, x1[:], s1[:])
+            y_ps.append(b)
+        x2 = sb("x2", [P, S], U32)
+        nc.vector.tensor_copy(x2[:], xw[:].indirect(two_t[:]))
+        w2_q = quantize_weight("w2", cast_weight("w2", w2_raw, "gg"))
+        c_ps = []
+        for t in range(PACK):
+            b = psum.tile([P, S], F32, name="c_ps%d" % t, tag="bank%d" % (PACK + t))
+            product(b[:], w2_q, t, x2[:], s2[:])
+            c_ps.append(b)
+
+        def window(name, bank, engine, tag=None):
+            win = sb(name + "_win", [P, S], F32, tag)
+            evacuate(engine, win[:], bank[:])
+            return win
+
+        def fetch(name, win, lst, engine):
+            got = sb(name + "_got", [P, S], F32)
+            for a in range(0, S, HALF):
+                gather(engine, got[:, a : a + HALF], win, cols(lst, a, HALF))
+            return got
+
+        def extreme(name, bank, got, op, tag=None):
+            res = sb(name, [P, S], F32, tag)
+            nc.vector.tensor_tensor(res[:], bank[:], got[:], op)
+            return res
+
+        REST = S - SLICE
+        p_gain = sb("p_gain", [P, PACK, REST], F32)
+        q_gain = sb("q_gain", [P, PACK, REST], F32)
+
+        def scale(dst, src, t):
+            nc.gpsimd.tensor_scalar(dst[:, t, :], src[:, SLICE:], gain[:, t : t + 1], 0.0, ALU.mult, ALU.add)
+
+        p_t, q_t = [None] * PACK, [None] * PACK
+        yg = [fetch("y%d" % t, window("y%d" % t, y_ps[t], "s", "y_win%d" % (t % 2)), n1_t, "s") for t in range(PACK)]
+        p_t[0] = extreme("p0", y_ps[0], yg[0], ALU.max, "w2_bf0")
+        cw0 = window("c0", c_ps[0], "v")
+        q_t[0] = extreme("q0", c_ps[0], fetch("c0", cw0, n2_t, "v"), ALU.min)
+        p_t[1] = extreme("p1", y_ps[1], yg[1], ALU.max, "c0_win")
+        cw1 = window("c1", c_ps[1], "v")
+        cw2 = window("c2", c_ps[2], "v")
+        cg1 = fetch("c1", cw1, n2_t, "v")
+        cw3 = window("c3", c_ps[3], "v")
+        q_t[1] = extreme("q1", c_ps[1], cg1, ALU.min)
+        p_t[2] = extreme("p2", y_ps[2], yg[2], ALU.max, "c1_win")
+        p_t[3] = extreme("p3", y_ps[3], yg[3], ALU.max, "c1_got")
+        w3_q = quantize_weight("w3", cast_weight("w3", w3_raw, "gg"))
+        q_t[2] = extreme("q2", c_ps[2], fetch("c2", cw2, n2_t, "s"), ALU.min)
+        q_t[3] = extreme("q3", c_ps[3], fetch("c3", cw3, n2_t, "s"), ALU.min)
+        for t in range(PACK):
+            scale(p_gain, p_t[t], t)
+            scale(q_gain, q_t[t], t)
+
+        def look_up(s, e_p, e_q, tag_p, tag_q):
+            a0 = s * SLICE
+            pg = sb("pg%d" % s, [P, PACK, SLICE], F32, tag_p)
+            qg = sb("qg%d" % s, [P, PACK, SLICE], F32, tag_q)
+            for t in range(PACK):
+                gather(e_p[t], pg[:, t, :], p_t[t], cols(n2_t, a0, SLICE))
+            for t in range(PACK):
+                gather(e_q[t], qg[:, t, :], q_t[t], cols(n1_t, a0, SLICE))
+            return pg, qg
+
+        def cross(s, pg, qg, tag=None):
+            a0 = s * SLICE
+            both = sb("both%d" % s, [P, 2, PACK, SLICE], F32, tag)
+            left, right = both[:, 0], both[:, 1]
+            if s == 0:
+                eng = nc.vector
+                for t in range(PACK):
+                    g = gain[:, t : t + 1]
+                    nc.vector.scalar_tensor_tensor(right[:, t, :], q_t[t][:, :SLICE], g, pg[:, t, :], ALU.mult, ALU.mult)
+                    nc.vector.scalar_tensor_tensor(left[:, t, :], p_t[t][:, :SLICE], g, qg[:, t, :], ALU.mult, ALU.mult)
+            else:
+                eng = nc.gpsimd
+                nc.gpsimd.tensor_tensor(right, q_gain[:, :, a0 - SLICE : a0], pg[:], ALU.mult)
+                nc.gpsimd.tensor_tensor(left, p_gain[:, :, a0 - SLICE : a0], qg[:], ALU.mult)
+            z = sb("z%d" % s, [P, SLICE * PACK], BF16)
+            walk = "p t (c i) -> p c t i"
+            eng.tensor_tensor(
+                z[:].rearrange("p (c i t) -> p c t i", i=4, t=PACK),
+                left.rearrange(walk, i=4), right.rearrange(walk, i=4), ALU.subtract,
+            )
+            return z
+
+        def layer(s, z):
+            codes = sb("z_codes%d" % s, [P, SLICE], U32)
+            scales = sb("z_scales%d" % s, [P, SLICE], U8)
+            nc.vector.quantize_mx(out=codes[:].bitcast(FP8X4), scales=scales[:], in_=z[:])
+            banks = []
+            for u in range(2):
+                bank = psum.tile([P, 2, SLICE], F32, name="h_ps%d_%d" % (s, u), tag="bank%d" % (2 * s + u))
+                for e in range(2):
+                    product(bank[:, e, :], w3_q, 2 * u + e, codes[:], scales[:])
+                banks.append(bank)
+            return banks
+
+        def put(s, u, bank, engine, tag):
+            h = sb("h%d_%d" % (s, u), [P, 2, SLICE], F32, tag)
+            evacuate(engine, h[:], bank[:])
+            for e in range(2):
+                nc.vector.tensor_copy(page[2 * u + e][:].indirect(cols(slot_t, s * SLICE, SLICE)), h[:, e, :])
+
+        g0 = look_up(0, "ssss", "vvvs", "c2_win", None)
+        banks0 = layer(0, cross(0, *g0))
+        g1 = look_up(1, "ssss", "vvvv", "c3_win", "both0")
+        z1 = cross(1, *g1)
+        g2 = look_up(2, "ssss", "ssss", "c2_win", "qg0")
+        put(0, 0, banks0[0], "v", None)
+        banks1 = layer(1, z1)
+        put(0, 1, banks0[1], "s", "both1")
+        z2 = cross(2, *g2, "both0")
+        put(1, 0, banks1[0], "s", None)
+        g3 = look_up(3, "ssss", "ssss", "z1", "both1")
+        banks2 = layer(2, z2)
+        put(1, 1, banks1[1], "s", "both0")
+        z3 = cross(3, *g3, "qg0")
+        put(2, 0, banks2[0], "s", None)
+        banks3 = layer(3, z3)
+        put(2, 1, banks2[1], "s", "qg0")
+        put(3, 0, banks3[0], "s", None)
+        put(3, 1, banks3[1], "s", None)
+        for t in range(PACK):
+            nc.sync.dma_start(out_rows[t], page[t][:])

@@ -48,15 +48,15 @@ def tile_picked_wedge2_none_p_kernel(
 
         xs = sb("xs", [P, T], U8)
         nc.vector.memset(xs[:].bitcast(I32), 0)
-        w1_raw = load_weight("w1", w1)
+        xw = sb("xw", [P, T], U32)
+        nc.sync.dma_start(xw[:].bitcast(I32), x_words[0].rearrange("p n t -> p (n t)").bitcast(I32))
         for q in range(4):
             nc.sync.dma_start(xs[32 * q : 32 * q + 4, :].bitcast(I32), x_scales[0, 4 * q : 4 * q + 4, :].bitcast(I32))
         offs_t = load_list("offs_t", offs)
-        xw = sb("xw", [P, T], U32)
-        nc.sync.dma_start(xw[:].bitcast(I32), x_words[0].rearrange("p n t -> p (n t)").bitcast(I32))
         two_t = load_list("two_t", two)
-        w2_raw = load_weight("w2", w2)
+        w1_raw = load_weight("w1", w1)
         n1_t = load_list("n1_t", n1)
+        w2_raw = load_weight("w2", w2)
         n2_t = load_list("n2_t", n2)
         w3_raw = load_weight("w3", w3)
         gain = sb("gain", [P, PACK], F32)
@@ -74,8 +74,9 @@ def tile_picked_wedge2_none_p_kernel(
             halves = []
             for u in range(2):
                 g = sb("%s_bf%d" % (name, u), [P, 2 * P * PACK], BF16)
-                dst = g[:].rearrange("p (t m j) -> p m t j", t=2, j=PACK)
-                src = raw[:].rearrange("p j (m t) -> p m t j", t=PACK)[:, :, 2 * u : 2 * u + 2, :]
+                order = "p m t j" if engines[u] == "g" else "p m j t"
+                dst = g[:].rearrange("p (t m j) -> " + order, t=2, j=PACK)
+                src = raw[:].rearrange("p j (m u t) -> p u m j t", u=2, t=2)[:, u].rearrange("p m j t -> " + order)
                 if engines[u] == "v":
                     nc.vector.tensor_copy(dst, src)
                 elif engines[u] == "g":
@@ -116,19 +117,19 @@ def tile_picked_wedge2_none_p_kernel(
 
         s1 = sb("s1", [P, S], U8)
         nc.vector.tensor_copy(s1[:], xs[:].indirect(offs_t[:]))
-        w1_q = quantize_weight("w1", cast_weight("w1", w1_raw, "vs"))
-        s2 = sb("s2", [P, S], U8)
-        nc.vector.tensor_copy(s2[:], xs[:].indirect(two_t[:]))
         x1 = sb("x1", [P, S], U32)
         nc.vector.tensor_copy(x1[:], xw[:].indirect(offs_t[:]))
+        s2 = sb("s2", [P, S], U8)
+        nc.vector.tensor_copy(s2[:], xs[:].indirect(two_t[:]))
+        w1_q = quantize_weight("w1", cast_weight("w1", w1_raw, "ss"))
         y_ps = []
         for t in range(PACK):
             b = psum.tile([P, S], F32, name="y_ps%d" % t, tag="bank%d" % t)
             product(b[:], w1_q, t, x1[:], s1[:])
             y_ps.append(b)
-        x2 = sb("x2", [P, S], U32)
+        x2 = sb("x2", [P, S], U32, "w1_bf0")
         nc.vector.tensor_copy(x2[:], xw[:].indirect(two_t[:]))
-        w2_q = quantize_weight("w2", cast_weight("w2", w2_raw, "gg"))
+        w2_q = quantize_weight("w2", cast_weight("w2", w2_raw, "vv"))
         c_ps = []
         for t in range(PACK):
             b = psum.tile([P, S], F32, name="c_ps%d" % t, tag="bank%d" % (PACK + t))
@@ -160,20 +161,30 @@ def tile_picked_wedge2_none_p_kernel(
 
         p_t, q_t = [None] * PACK, [None] * PACK
         yg = [fetch("y%d" % t, window("y%d" % t, y_ps[t], "s", "y_win%d" % (t % 2)), n1_t, "s") for t in range(PACK)]
-        p_t[0] = extreme("p0", y_ps[0], yg[0], ALU.max, "w2_bf0")
+        p_t[0] = extreme("p0", y_ps[0], yg[0], ALU.max, "w2_raw")
         cw0 = window("c0", c_ps[0], "v")
+        cw1 = window("c1", c_ps[1], "v")
         q_t[0] = extreme("q0", c_ps[0], fetch("c0", cw0, n2_t, "v"), ALU.min)
         p_t[1] = extreme("p1", y_ps[1], yg[1], ALU.max, "c0_win")
-        cw1 = window("c1", c_ps[1], "v")
-        cw2 = window("c2", c_ps[2], "v")
-        cg1 = fetch("c1", cw1, n2_t, "v")
-        cw3 = window("c3", c_ps[3], "v")
-        q_t[1] = extreme("q1", c_ps[1], cg1, ALU.min)
+        q_t[1] = extreme("q1", c_ps[1], fetch("c1", cw1, n2_t, "v"), ALU.min)
         p_t[2] = extreme("p2", y_ps[2], yg[2], ALU.max, "c1_win")
         p_t[3] = extreme("p3", y_ps[3], yg[3], ALU.max, "c1_got")
-        w3_q = quantize_weight("w3", cast_weight("w3", w3_raw, "gg"))
-        q_t[2] = extreme("q2", c_ps[2], fetch("c2", cw2, n2_t, "s"), ALU.min)
-        q_t[3] = extreme("q3", c_ps[3], fetch("c3", cw3, n2_t, "s"), ALU.min)
+        w3_bf = sb("w3_bf", [P, PACK * P * PACK], BF16, "w2_bf1")
+        nc.gpsimd.tensor_scalar(
+            w3_bf[:].rearrange("p (t m j) -> p m t j", t=PACK, j=PACK),
+            w3_raw[:].rearrange("p j (m t) -> p m t j", t=PACK), 1.0, 0.0, ALU.mult, ALU.add,
+        )
+        w3_codes = sb("w3_codes", [P, PACK * P], U32)
+        w3_scales = sb("w3_scales", [P, PACK * P], U8)
+        nc.vector.quantize_mx(out=w3_codes[:].bitcast(FP8X4), scales=w3_scales[:], in_=w3_bf[:])
+        w3_q = [(w3_codes[:, : 2 * P], w3_scales[:, : 2 * P]), (w3_codes[:, 2 * P :], w3_scales[:, 2 * P :])]
+        q_t[2] = extreme("q2", c_ps[2], fetch("c2", window("c2", c_ps[2], "s", "y_win0"), n2_t, "s"), ALU.min, "w2_bf1")
+        cg3 = fetch("c3", window("c3", c_ps[3], "s", "y_win1"), n2_t, "s")
+        qg0 = sb("qg0", [P, PACK, SLICE], F32)
+        for t in range(PACK):
+            if t == 3:
+                q_t[3] = extreme("q3", c_ps[3], cg3, ALU.min, "c2_got")
+            gather("v", qg0[:, t, :], q_t[t], cols(n1_t, 0, SLICE))
         for t in range(PACK):
             scale(p_gain, p_t[t], t)
             scale(q_gain, q_t[t], t)
@@ -188,10 +199,14 @@ def tile_picked_wedge2_none_p_kernel(
                 gather(e_q[t], qg[:, t, :], q_t[t], cols(n1_t, a0, SLICE))
             return pg, qg
 
-        def cross(s, pg, qg, tag=None):
+        def cross(s, pg, qg, tag_r=None, tag_l=None):
             a0 = s * SLICE
-            both = sb("both%d" % s, [P, 2, PACK, SLICE], F32, tag)
-            left, right = both[:, 0], both[:, 1]
+            if s < 2:
+                right = sb("right%d" % s, [P, PACK, SLICE], F32, tag_r)[:]
+                left = sb("left%d" % s, [P, PACK, SLICE], F32, tag_l)[:]
+            else:
+                both = sb("both%d" % s, [P, 2, PACK, SLICE], F32, tag_r)
+                left, right = both[:, 0], both[:, 1]
             if s == 0:
                 eng = nc.vector
                 for t in range(PACK):
@@ -200,52 +215,69 @@ def tile_picked_wedge2_none_p_kernel(
                     nc.vector.scalar_tensor_tensor(left[:, t, :], p_t[t][:, :SLICE], g, qg[:, t, :], ALU.mult, ALU.mult)
             else:
                 eng = nc.gpsimd
-                nc.gpsimd.tensor_tensor(right, q_gain[:, :, a0 - SLICE : a0], pg[:], ALU.mult)
+                (nc.vector if s == 1 else nc.gpsimd).tensor_tensor(right, q_gain[:, :, a0 - SLICE : a0], pg[:], ALU.mult)
                 nc.gpsimd.tensor_tensor(left, p_gain[:, :, a0 - SLICE : a0], qg[:], ALU.mult)
             z = sb("z%d" % s, [P, SLICE * PACK], BF16)
             walk = "p t (c i) -> p c t i"
             eng.tensor_tensor(
-                z[:].rearrange("p (c i t) -> p c t i", i=4, t=PACK),
-                left.rearrange(walk, i=4), right.rearrange(walk, i=4), ALU.subtract,
+                z[:].rearrange("p (c i t) -> p c t i", i=2, t=PACK),
+                left.rearrange(walk, i=2), right.rearrange(walk, i=2), ALU.subtract,
             )
             return z
 
-        def layer(s, z):
+        def layer(s, z, places):
             codes = sb("z_codes%d" % s, [P, SLICE], U32)
             scales = sb("z_scales%d" % s, [P, SLICE], U8)
             nc.vector.quantize_mx(out=codes[:].bitcast(FP8X4), scales=scales[:], in_=z[:])
-            banks = []
-            for u in range(2):
-                bank = psum.tile([P, 2, SLICE], F32, name="h_ps%d_%d" % (s, u), tag="bank%d" % (2 * s + u))
-                for e in range(2):
-                    product(bank[:, e, :], w3_q, 2 * u + e, codes[:], scales[:])
-                banks.append(bank)
-            return banks
+            for t in range(PACK):
+                product(places[t], w3_q, t, codes[:], scales[:])
 
-        def put(s, u, bank, engine, tag):
-            h = sb("h%d_%d" % (s, u), [P, 2, SLICE], F32, tag)
-            evacuate(engine, h[:], bank[:])
+        def bank(name, n, parts):
+            return psum.tile([P, parts, SLICE], F32, name=name, tag="bank%d" % n)
+
+        def leave(name, src, parts, engine, tag=None):
+            h = sb(name, [P, parts, SLICE], F32, tag)
+            evacuate(engine, h[:], src[:])
+            return h
+
+        def put(t, start, count, values):
+            nc.vector.tensor_copy(page[t][:].indirect(cols(slot_t, start, count)), values)
+
+        def put_pair(s, u, src, engine, tag=None):
+            h = leave("h%d_%d" % (s, u), src, 2, engine, tag)
             for e in range(2):
-                nc.vector.tensor_copy(page[2 * u + e][:].indirect(cols(slot_t, s * SLICE, SLICE)), h[:, e, :])
+                put(2 * u + e, s * SLICE, SLICE, h[:, e, :])
 
-        g0 = look_up(0, "ssss", "vvvs", "c2_win", None)
-        banks0 = layer(0, cross(0, *g0))
-        g1 = look_up(1, "ssss", "vvvv", "c3_win", "both0")
-        z1 = cross(1, *g1)
-        g2 = look_up(2, "ssss", "ssss", "c2_win", "qg0")
-        put(0, 0, banks0[0], "v", None)
-        banks1 = layer(1, z1)
-        put(0, 1, banks0[1], "s", "both1")
-        z2 = cross(2, *g2, "both0")
-        put(1, 0, banks1[0], "s", None)
-        g3 = look_up(3, "ssss", "ssss", "z1", "both1")
-        banks2 = layer(2, z2)
-        put(1, 1, banks1[1], "s", "both0")
-        z3 = cross(3, *g3, "qg0")
-        put(2, 0, banks2[0], "s", None)
-        banks3 = layer(3, z3)
-        put(2, 1, banks2[1], "s", "qg0")
-        put(3, 0, banks3[0], "s", None)
-        put(3, 1, banks3[1], "s", None)
+        def pairs(s):
+            a, b = bank("h_ps%d_0" % s, 2 * s, 2), bank("h_ps%d_1" % s, 2 * s + 1, 2)
+            return a, b, [a[:, 0, :], a[:, 1, :], b[:, 0, :], b[:, 1, :]]
+
+        pg0 = sb("pg0", [P, PACK, SLICE], F32, "y_win0")
+        for t in range(PACK):
+            gather("s", pg0[:, t, :], p_t[t], cols(n2_t, 0, SLICE))
+        g0 = (pg0, qg0)
+        a0, b0, places = pairs(0)
+        layer(0, cross(0, *g0), places)
+        g1 = look_up(1, "ssss", "ssss", "y_win1", "c3_got")
+        z1 = cross(1, *g1, "z0", "y_win1")
+        g2 = look_up(2, "ssss", "ssss", "y_win0", "qg0")
+        put_pair(0, 0, a0, "v")
+        a1, b1, places = pairs(1)
+        layer(1, z1, places)
+        put_pair(0, 1, b0, "s", "z0")
+        z2 = cross(2, *g2, "z1", "y_win1")
+        put_pair(1, 0, a1, "s")
+        g3 = look_up(3, "ssss", "ssss", "z_codes1", "z_scales1")
+        a2, b2, last = bank("h_ps2_0", 4, 2), bank("h_ps2_2", 5, 1), bank("h_last", 6, 2)
+        layer(2, z2, [a2[:, 0, :], a2[:, 1, :], b2[:, 0, :], last[:, 0, :]])
+        put_pair(1, 1, b1, "s", "z1")
+        z3 = cross(3, *g3, "z2", "y_win1")
+        put_pair(2, 0, a2, "s")
+        a3, b3 = bank("h_ps3_0", 7, 2), bank("h_ps3_2", 0, 1)
+        layer(3, z3, [a3[:, 0, :], a3[:, 1, :], b3[:, 0, :], last[:, 1, :]])
+        put(2, 2 * SLICE, SLICE, leave("h2_2", b2, 1, "s", "z2")[:, 0, :])
+        put_pair(3, 0, a3, "s")
+        put(2, 3 * SLICE, SLICE, leave("h3_2", b3, 1, "s")[:, 0, :])
+        put(3, 2 * SLICE, 2 * SLICE, leave("h_last_sb", last, 2, "s")[:].rearrange("p a b -> p (a b)"))
         for t in range(PACK):
             nc.sync.dma_start(out_rows[t], page[t][:])

@@ -49,12 +49,14 @@ def tile_picked_wedge2_none_p_kernel(
         xs = sb("xs", [P, T], U8)
         nc.vector.memset(xs[:].bitcast(I32), 0)
         xw = sb("xw", [P, T], U32)
-        nc.sync.dma_start(xw[:].bitcast(I32), x_words[0].rearrange("p n t -> p (n t)").bitcast(I32))
+        xw_rows = x_words[0].rearrange("p n t -> p (n t)").bitcast(I32)
+        nc.sync.dma_start(xw[:, : T // 2].bitcast(I32), xw_rows[:, : T // 2])
         for q in range(4):
-            nc.sync.dma_start(xs[32 * q : 32 * q + 4, :].bitcast(I32), x_scales[0, 4 * q : 4 * q + 4, :].bitcast(I32))
+            nc.sync.dma_start(xs[q:P:32, :].bitcast(I32), x_scales[0, q:16:4, :].bitcast(I32))
         offs_t = load_list("offs_t", offs)
         two_t = load_list("two_t", two)
         w1_raw = load_weight("w1", w1)
+        nc.sync.dma_start(xw[:, T // 2 :].bitcast(I32), xw_rows[:, T // 2 :])
         n1_t = load_list("n1_t", n1)
         w2_raw = load_weight("w2", w2)
         n2_t = load_list("n2_t", n2)
@@ -88,7 +90,7 @@ def tile_picked_wedge2_none_p_kernel(
 
         def quantize_weight(name, halves):
             made = []
-            for u in range(2):
+            for u in range(len(halves)):
                 codes = sb("%s_codes%d" % (name, u), [P, 2 * P], U32)
                 scales = sb("%s_scales%d" % (name, u), [P, 2 * P], U8)
                 nc.vector.quantize_mx(out=codes[:].bitcast(FP8X4), scales=scales[:], in_=halves[u][:])
@@ -117,11 +119,13 @@ def tile_picked_wedge2_none_p_kernel(
 
         s1 = sb("s1", [P, S], U8)
         nc.vector.tensor_copy(s1[:], xs[:].indirect(offs_t[:]))
-        x1 = sb("x1", [P, S], U32)
-        nc.vector.tensor_copy(x1[:], xw[:].indirect(offs_t[:]))
         s2 = sb("s2", [P, S], U8)
         nc.vector.tensor_copy(s2[:], xs[:].indirect(two_t[:]))
-        w1_q = quantize_weight("w1", cast_weight("w1", w1_raw, "ss"))
+        w1_bf = cast_weight("w1", w1_raw, "ss")
+        w1_q = quantize_weight("w1", w1_bf[:1])
+        x1 = sb("x1", [P, S], U32)
+        nc.vector.tensor_copy(x1[:], xw[:].indirect(offs_t[:]))
+        w1_q = w1_q + quantize_weight("w1b", w1_bf[1:])
         y_ps = []
         for t in range(PACK):
             b = psum.tile([P, S], F32, name="y_ps%d" % t, tag="bank%d" % t)
@@ -161,9 +165,9 @@ def tile_picked_wedge2_none_p_kernel(
 
         p_t, q_t = [None] * PACK, [None] * PACK
         yg = [fetch("y%d" % t, window("y%d" % t, y_ps[t], "s", "y_win%d" % (t % 2)), n1_t, "s") for t in range(PACK)]
-        p_t[0] = extreme("p0", y_ps[0], yg[0], ALU.max, "w2_raw")
         cw0 = window("c0", c_ps[0], "v")
         cw1 = window("c1", c_ps[1], "v")
+        p_t[0] = extreme("p0", y_ps[0], yg[0], ALU.max, "w2_bf0")
         q_t[0] = extreme("q0", c_ps[0], fetch("c0", cw0, n2_t, "v"), ALU.min)
         p_t[1] = extreme("p1", y_ps[1], yg[1], ALU.max, "c0_win")
         q_t[1] = extreme("q1", c_ps[1], fetch("c1", cw1, n2_t, "v"), ALU.min)
@@ -201,12 +205,8 @@ def tile_picked_wedge2_none_p_kernel(
 
         def cross(s, pg, qg, tag_r=None, tag_l=None):
             a0 = s * SLICE
-            if s < 2:
-                right = sb("right%d" % s, [P, PACK, SLICE], F32, tag_r)[:]
-                left = sb("left%d" % s, [P, PACK, SLICE], F32, tag_l)[:]
-            else:
-                both = sb("both%d" % s, [P, 2, PACK, SLICE], F32, tag_r)
-                left, right = both[:, 0], both[:, 1]
+            right = sb("right%d" % s, [P, PACK, SLICE], F32, tag_r)[:]
+            left = sb("left%d" % s, [P, PACK, SLICE], F32, tag_l)[:]
             if s == 0:
                 eng = nc.vector
                 for t in range(PACK):
@@ -216,7 +216,7 @@ def tile_picked_wedge2_none_p_kernel(
             else:
                 eng = nc.gpsimd
                 (nc.vector if s == 1 else nc.gpsimd).tensor_tensor(right, q_gain[:, :, a0 - SLICE : a0], pg[:], ALU.mult)
-                nc.gpsimd.tensor_tensor(left, p_gain[:, :, a0 - SLICE : a0], qg[:], ALU.mult)
+                (nc.vector if s == 1 else nc.gpsimd).tensor_tensor(left, p_gain[:, :, a0 - SLICE : a0], qg[:], ALU.mult)
             z = sb("z%d" % s, [P, SLICE * PACK], BF16)
             walk = "p t (c i) -> p c t i"
             eng.tensor_tensor(
@@ -260,18 +260,18 @@ def tile_picked_wedge2_none_p_kernel(
         layer(0, cross(0, *g0), places)
         g1 = look_up(1, "ssss", "ssss", "y_win1", "c3_got")
         z1 = cross(1, *g1, "z0", "y_win1")
-        g2 = look_up(2, "ssss", "ssss", "y_win0", "qg0")
-        put_pair(0, 0, a0, "v")
+        put_pair(0, 0, a0, "s")
+        g2 = look_up(2, "ssss", "ssss", "y_win0", "z_codes0")
         a1, b1, places = pairs(1)
         layer(1, z1, places)
         put_pair(0, 1, b0, "s", "z0")
-        z2 = cross(2, *g2, "z1", "y_win1")
+        z2 = cross(2, *g2, "c3_got", "z1")
         put_pair(1, 0, a1, "s")
-        g3 = look_up(3, "ssss", "ssss", "z_codes1", "z_scales1")
+        g3 = look_up(3, "ssss", "ssss", "y_win1", "z_codes1")
         a2, b2, last = bank("h_ps2_0", 4, 2), bank("h_ps2_2", 5, 1), bank("h_last", 6, 2)
         layer(2, z2, [a2[:, 0, :], a2[:, 1, :], b2[:, 0, :], last[:, 0, :]])
         put_pair(1, 1, b1, "s", "z1")
-        z3 = cross(3, *g3, "z2", "y_win1")
+        z3 = cross(3, *g3, "z_codes0", "z2")
         put_pair(2, 0, a2, "s")
         a3, b3 = bank("h_ps3_0", 7, 2), bank("h_ps3_2", 0, 1)
         layer(3, z3, [a3[:, 0, :], a3[:, 1, :], b3[:, 0, :], last[:, 1, :]])

@@ -2,8 +2,9 @@ from contextlib import ExitStack
 
 import concourse.mybir as mybir
 
-K, T, S, N, H, U = 512, 2048, 512, 512, 512, 1024
-FLOPS = 3 * 2 * 512 * 512 * 512
+T, S, U = 2048, 512, 1024
+WIDTH = 512
+FLOPS = 3 * 2 * WIDTH * WIDTH * S
 
 F32 = mybir.dt.float32
 BF16 = mybir.dt.bfloat16
@@ -19,7 +20,7 @@ P = 128
 PACK = 4
 HALF = S // 2
 SLICE = 128
-SLICES = S // SLICE
+REST = S - SLICE
 
 
 def tile_picked_wedge2_none_p_kernel(
@@ -30,29 +31,35 @@ def tile_picked_wedge2_none_p_kernel(
         keep = ctx.enter_context(tc.tile_pool(name="keep", bufs=1))
         psum = ctx.enter_context(tc.psum_pool(name="psum", bufs=1))
 
-        def sb(name, shape, dtype, tag=None):
-            return keep.tile(shape, dtype, name=name, tag=tag or name, align_bytes=64)
+        def sb(name, shape, dtype, after=None):
+            return keep.tile(shape, dtype, name=name, tag=after or name, align_bytes=64)
 
         def load_list(name, src):
-            t = keep.tile([P, S // 16], U16, name=name)
-            nc.sync.dma_start(t[:], src)
-            return t
+            held = keep.tile([P, S // 16], U16, name=name)
+            nc.sync.dma_start(held[:], src)
+            return held
 
-        def cols(lst, start, count):
+        def entries(lst, start, count):
             return lst[:, start // 16 : (start + count) // 16]
 
         def load_weight(name, w):
-            raw = sb(name + "_raw", [P, PACK, 512], F32)
+            raw = sb(name + "_raw", [P, PACK, WIDTH], F32)
             nc.sync.dma_start(raw[:], w.rearrange("(p j) c -> p j c", j=PACK))
             return raw
+
+        def vector_gather(dst, window, offsets):
+            nc.vector.tensor_copy(dst, window[:].indirect(offsets))
+
+        def scalar_gather(dst, window, offsets):
+            nc.scalar.activation(dst, window[:].indirect(offsets), COPY)
 
         xs = sb("xs", [P, T], U8)
         nc.vector.memset(xs[:].bitcast(I32), 0)
         xw = sb("xw", [P, T], U32)
         xw_rows = x_words[0].rearrange("p n t -> p (n t)").bitcast(I32)
         nc.sync.dma_start(xw[:, : T // 2].bitcast(I32), xw_rows[:, : T // 2])
-        for q in range(4):
-            nc.sync.dma_start(xs[q:P:32, :].bitcast(I32), x_scales[0, q:16:4, :].bitcast(I32))
+        for r in range(4):
+            nc.sync.dma_start(xs[r:P:32, :].bitcast(I32), x_scales[0, r:16:4, :].bitcast(I32))
         offs_t = load_list("offs_t", offs)
         two_t = load_list("two_t", two)
         w1_raw = load_weight("w1", w1)
@@ -64,220 +71,206 @@ def tile_picked_wedge2_none_p_kernel(
         gain = sb("gain", [P, PACK], F32)
         nc.sync.dma_start(gain[:], gn.rearrange("(p t) o -> p (t o)", t=PACK))
         slot_t = load_list("slot_t", slot)
-        page = []
         mem_rows = mem.rearrange("(p t) u -> t p u", t=PACK)
         out_rows = out.rearrange("(p t) u -> t p u", t=PACK)
+        page = []
         for t in range(PACK):
-            pg = sb("page%d" % t, [P, U], F32)
-            nc.sync.dma_start(pg[:], mem_rows[t])
-            page.append(pg)
+            page.append(sb("page%d" % t, [P, U], F32))
+            nc.sync.dma_start(page[t][:], mem_rows[t])
 
-        def cast_weight(name, raw, engines):
+        def round_halves(name, raw, copy):
             halves = []
             for u in range(2):
-                g = sb("%s_bf%d" % (name, u), [P, 2 * P * PACK], BF16)
-                order = "p m t j" if engines[u] == "g" else "p m j t"
-                dst = g[:].rearrange("p (t m j) -> " + order, t=2, j=PACK)
-                src = raw[:].rearrange("p j (m u t) -> p u m j t", u=2, t=2)[:, u].rearrange("p m j t -> " + order)
-                if engines[u] == "v":
-                    nc.vector.tensor_copy(dst, src)
-                elif engines[u] == "g":
-                    nc.gpsimd.tensor_scalar(dst, src, 1.0, 0.0, ALU.mult, ALU.add)
-                else:
-                    nc.scalar.copy(dst, src)
-                halves.append(g)
+                half = sb("%s_bf%d" % (name, u), [P, 2 * P * PACK], BF16)
+                src = raw[:].rearrange("p j (m u t) -> p u m j t", u=2, t=2)[:, u]
+                copy(half[:].rearrange("p (t m j) -> p m j t", t=2, j=PACK), src)
+                halves.append(half)
             return halves
 
-        def quantize_weight(name, halves):
-            made = []
-            for u in range(len(halves)):
-                codes = sb("%s_codes%d" % (name, u), [P, 2 * P], U32)
-                scales = sb("%s_scales%d" % (name, u), [P, 2 * P], U8)
-                nc.vector.quantize_mx(out=codes[:].bitcast(FP8X4), scales=scales[:], in_=halves[u][:])
-                made.append((codes, scales))
-            return made
+        def quantize(name, values, words):
+            codes = sb(name % "codes", [P, words], U32)
+            scales = sb(name % "scales", [P, words], U8)
+            nc.vector.quantize_mx(out=codes[:].bitcast(FP8X4), scales=scales[:], in_=values[:])
+            return codes, scales
 
-        def product(dst, wq, t, codes, scales):
-            wc, ws = wq[t // 2]
+        def product(dst, weight_halves, t, codes, scales):
+            w_codes, w_scales = weight_halves[t // 2]
             m = slice((t % 2) * P, (t % 2 + 1) * P)
             nc.tensor.matmul_mx(
-                out=dst, lhsT=wc[:, m].bitcast(FP8X4), lhsT_scale=ws[:, m],
-                rhs=codes.bitcast(FP8X4), rhs_scale=scales, start=True, stop=True,
+                out=dst, lhsT=w_codes[:, m].bitcast(FP8X4), lhsT_scale=w_scales[:, m],
+                rhs=codes[:].bitcast(FP8X4), rhs_scale=scales[:], start=True, stop=True,
             )
 
-        def gather(engine, dst, window, offsets):
-            if engine == "v":
-                nc.vector.tensor_copy(dst, window[:].indirect(offsets))
-            else:
-                nc.scalar.activation(dst, window[:].indirect(offsets), COPY)
-
-        def evacuate(engine, dst, src):
-            if engine == "v":
-                nc.vector.tensor_copy(dst, src)
-            else:
-                nc.scalar.copy(dst, src)
+        def projection(name, first_bank, weight_halves, codes, scales):
+            banks = []
+            for t in range(PACK):
+                banks.append(psum.tile([P, S], F32, name="%s_ps%d" % (name, t), tag="bank%d" % (first_bank + t)))
+                product(banks[t][:], weight_halves, t, codes, scales)
+            return banks
 
         s1 = sb("s1", [P, S], U8)
-        nc.vector.tensor_copy(s1[:], xs[:].indirect(offs_t[:]))
+        vector_gather(s1[:], xs, offs_t[:])
         s2 = sb("s2", [P, S], U8)
-        nc.vector.tensor_copy(s2[:], xs[:].indirect(two_t[:]))
-        w1_bf = cast_weight("w1", w1_raw, "ss")
-        w1_q = quantize_weight("w1", w1_bf[:1])
+        vector_gather(s2[:], xs, two_t[:])
+        w1_bf = round_halves("w1", w1_raw, nc.scalar.copy)
+        w1_q = [quantize("w1_%s0", w1_bf[0], 2 * P)]
         x1 = sb("x1", [P, S], U32)
-        nc.vector.tensor_copy(x1[:], xw[:].indirect(offs_t[:]))
-        w1_q = w1_q + quantize_weight("w1b", w1_bf[1:])
-        y_ps = []
-        for t in range(PACK):
-            b = psum.tile([P, S], F32, name="y_ps%d" % t, tag="bank%d" % t)
-            product(b[:], w1_q, t, x1[:], s1[:])
-            y_ps.append(b)
-        x2 = sb("x2", [P, S], U32, "w1_bf0")
-        nc.vector.tensor_copy(x2[:], xw[:].indirect(two_t[:]))
-        w2_q = quantize_weight("w2", cast_weight("w2", w2_raw, "vv"))
-        c_ps = []
-        for t in range(PACK):
-            b = psum.tile([P, S], F32, name="c_ps%d" % t, tag="bank%d" % (PACK + t))
-            product(b[:], w2_q, t, x2[:], s2[:])
-            c_ps.append(b)
+        vector_gather(x1[:], xw, offs_t[:])
+        w1_q.append(quantize("w1b_%s0", w1_bf[1], 2 * P))
+        y_ps = projection("y", 0, w1_q, x1, s1)
+        x2 = sb("x2", [P, S], U32, after="w1_bf0")
+        vector_gather(x2[:], xw, two_t[:])
+        w2_bf = round_halves("w2", w2_raw, nc.vector.tensor_copy)
+        w2_q = [quantize("w2_%%s%d" % u, w2_bf[u], 2 * P) for u in range(2)]
+        c_ps = projection("c", PACK, w2_q, x2, s2)
 
-        def window(name, bank, engine, tag=None):
-            win = sb(name + "_win", [P, S], F32, tag)
-            evacuate(engine, win[:], bank[:])
+        def window(name, bank, copy, after=None):
+            win = sb(name + "_win", [P, S], F32, after)
+            copy(win[:], bank[:])
             return win
 
-        def fetch(name, win, lst, engine):
+        def fetch(name, win, lst, gather):
             got = sb(name + "_got", [P, S], F32)
-            for a in range(0, S, HALF):
-                gather(engine, got[:, a : a + HALF], win, cols(lst, a, HALF))
+            for start in range(0, S, HALF):
+                gather(got[:, start : start + HALF], win, entries(lst, start, HALF))
             return got
 
-        def extreme(name, bank, got, op, tag=None):
-            res = sb(name, [P, S], F32, tag)
+        def extreme(name, bank, got, op, after=None):
+            res = sb(name, [P, S], F32, after)
             nc.vector.tensor_tensor(res[:], bank[:], got[:], op)
             return res
 
-        REST = S - SLICE
         p_gain = sb("p_gain", [P, PACK, REST], F32)
         q_gain = sb("q_gain", [P, PACK, REST], F32)
 
-        def scale(dst, src, t):
-            nc.gpsimd.tensor_scalar(dst[:, t, :], src[:, SLICE:], gain[:, t : t + 1], 0.0, ALU.mult, ALU.add)
+        p, q = [None] * PACK, [None] * PACK
+        y_got = []
+        for t in range(PACK):
+            y_win = window("y%d" % t, y_ps[t], nc.scalar.copy, after="y_win%d" % (t % 2))
+            y_got.append(fetch("y%d" % t, y_win, n1_t, scalar_gather))
+        c0_win = window("c0", c_ps[0], nc.vector.tensor_copy)
+        c1_win = window("c1", c_ps[1], nc.vector.tensor_copy)
+        p[0] = extreme("p0", y_ps[0], y_got[0], ALU.max, after="w2_bf0")
+        q[0] = extreme("q0", c_ps[0], fetch("c0", c0_win, n2_t, vector_gather), ALU.min)
+        p[1] = extreme("p1", y_ps[1], y_got[1], ALU.max, after="c0_win")
+        q[1] = extreme("q1", c_ps[1], fetch("c1", c1_win, n2_t, vector_gather), ALU.min)
+        p[2] = extreme("p2", y_ps[2], y_got[2], ALU.max, after="c1_win")
+        p[3] = extreme("p3", y_ps[3], y_got[3], ALU.max, after="c1_got")
 
-        p_t, q_t = [None] * PACK, [None] * PACK
-        yg = [fetch("y%d" % t, window("y%d" % t, y_ps[t], "s", "y_win%d" % (t % 2)), n1_t, "s") for t in range(PACK)]
-        cw0 = window("c0", c_ps[0], "v")
-        cw1 = window("c1", c_ps[1], "v")
-        p_t[0] = extreme("p0", y_ps[0], yg[0], ALU.max, "w2_bf0")
-        q_t[0] = extreme("q0", c_ps[0], fetch("c0", cw0, n2_t, "v"), ALU.min)
-        p_t[1] = extreme("p1", y_ps[1], yg[1], ALU.max, "c0_win")
-        q_t[1] = extreme("q1", c_ps[1], fetch("c1", cw1, n2_t, "v"), ALU.min)
-        p_t[2] = extreme("p2", y_ps[2], yg[2], ALU.max, "c1_win")
-        p_t[3] = extreme("p3", y_ps[3], yg[3], ALU.max, "c1_got")
-        w3_bf = sb("w3_bf", [P, PACK * P * PACK], BF16, "w2_bf1")
+        w3_bf = sb("w3_bf", [P, PACK * P * PACK], BF16, after="w2_bf1")
         nc.gpsimd.tensor_scalar(
             w3_bf[:].rearrange("p (t m j) -> p m t j", t=PACK, j=PACK),
             w3_raw[:].rearrange("p j (m t) -> p m t j", t=PACK), 1.0, 0.0, ALU.mult, ALU.add,
         )
-        w3_codes = sb("w3_codes", [P, PACK * P], U32)
-        w3_scales = sb("w3_scales", [P, PACK * P], U8)
-        nc.vector.quantize_mx(out=w3_codes[:].bitcast(FP8X4), scales=w3_scales[:], in_=w3_bf[:])
+        w3_codes, w3_scales = quantize("w3_%s", w3_bf, PACK * P)
         w3_q = [(w3_codes[:, : 2 * P], w3_scales[:, : 2 * P]), (w3_codes[:, 2 * P :], w3_scales[:, 2 * P :])]
-        q_t[2] = extreme("q2", c_ps[2], fetch("c2", window("c2", c_ps[2], "s", "y_win0"), n2_t, "s"), ALU.min, "w2_bf1")
-        cg3 = fetch("c3", window("c3", c_ps[3], "s", "y_win1"), n2_t, "s")
+
+        c2_win = window("c2", c_ps[2], nc.scalar.copy, after="y_win0")
+        q[2] = extreme("q2", c_ps[2], fetch("c2", c2_win, n2_t, scalar_gather), ALU.min, after="w2_bf1")
+        c3_win = window("c3", c_ps[3], nc.scalar.copy, after="y_win1")
+        c3_got = fetch("c3", c3_win, n2_t, scalar_gather)
         qg0 = sb("qg0", [P, PACK, SLICE], F32)
+        for t in range(PACK - 1):
+            vector_gather(qg0[:, t, :], q[t], entries(n1_t, 0, SLICE))
+        q[3] = extreme("q3", c_ps[3], c3_got, ALU.min, after="c2_got")
+        vector_gather(qg0[:, 3, :], q[3], entries(n1_t, 0, SLICE))
         for t in range(PACK):
-            if t == 3:
-                q_t[3] = extreme("q3", c_ps[3], cg3, ALU.min, "c2_got")
-            gather("v", qg0[:, t, :], q_t[t], cols(n1_t, 0, SLICE))
-        for t in range(PACK):
-            scale(p_gain, p_t[t], t)
-            scale(q_gain, q_t[t], t)
+            for dst, src in ((p_gain, p[t]), (q_gain, q[t])):
+                nc.gpsimd.tensor_scalar(dst[:, t, :], src[:, SLICE:], gain[:, t : t + 1], 0.0, ALU.mult, ALU.add)
 
-        def look_up(s, e_p, e_q, tag_p, tag_q):
-            a0 = s * SLICE
-            pg = sb("pg%d" % s, [P, PACK, SLICE], F32, tag_p)
-            qg = sb("qg%d" % s, [P, PACK, SLICE], F32, tag_q)
+        def look_up(name, tiles, lst, s, after):
+            got = sb("%s%d" % (name, s), [P, PACK, SLICE], F32, after)
             for t in range(PACK):
-                gather(e_p[t], pg[:, t, :], p_t[t], cols(n2_t, a0, SLICE))
-            for t in range(PACK):
-                gather(e_q[t], qg[:, t, :], q_t[t], cols(n1_t, a0, SLICE))
-            return pg, qg
+                scalar_gather(got[:, t, :], tiles[t], entries(lst, s * SLICE, SLICE))
+            return got
 
-        def cross(s, pg, qg, tag_r=None, tag_l=None):
-            a0 = s * SLICE
-            right = sb("right%d" % s, [P, PACK, SLICE], F32, tag_r)[:]
-            left = sb("left%d" % s, [P, PACK, SLICE], F32, tag_l)[:]
-            if s == 0:
-                eng = nc.vector
-                for t in range(PACK):
-                    g = gain[:, t : t + 1]
-                    nc.vector.scalar_tensor_tensor(right[:, t, :], q_t[t][:, :SLICE], g, pg[:, t, :], ALU.mult, ALU.mult)
-                    nc.vector.scalar_tensor_tensor(left[:, t, :], p_t[t][:, :SLICE], g, qg[:, t, :], ALU.mult, ALU.mult)
-            else:
-                eng = nc.gpsimd
-                (nc.vector if s == 1 else nc.gpsimd).tensor_tensor(right, q_gain[:, :, a0 - SLICE : a0], pg[:], ALU.mult)
-                (nc.vector if s == 1 else nc.gpsimd).tensor_tensor(left, p_gain[:, :, a0 - SLICE : a0], qg[:], ALU.mult)
+        def sides(s, right_after=None, left_after=None):
+            right = sb("right%d" % s, [P, PACK, SLICE], F32, right_after)
+            left = sb("left%d" % s, [P, PACK, SLICE], F32, left_after)
+            return right, left
+
+        def times(engine, dst, scaled, got, s):
+            engine.tensor_tensor(dst[:], scaled[:, :, (s - 1) * SLICE : s * SLICE], got[:], ALU.mult)
+
+        def difference(engine, s, left, right):
             z = sb("z%d" % s, [P, SLICE * PACK], BF16)
             walk = "p t (c i) -> p c t i"
-            eng.tensor_tensor(
+            engine.tensor_tensor(
                 z[:].rearrange("p (c i t) -> p c t i", i=2, t=PACK),
-                left.rearrange(walk, i=2), right.rearrange(walk, i=2), ALU.subtract,
+                left[:].rearrange(walk, i=2), right[:].rearrange(walk, i=2), ALU.subtract,
             )
             return z
 
         def layer(s, z, places):
-            codes = sb("z_codes%d" % s, [P, SLICE], U32)
-            scales = sb("z_scales%d" % s, [P, SLICE], U8)
-            nc.vector.quantize_mx(out=codes[:].bitcast(FP8X4), scales=scales[:], in_=z[:])
+            codes, scales = quantize("z_%%s%d" % s, z, SLICE)
             for t in range(PACK):
-                product(places[t], w3_q, t, codes[:], scales[:])
+                product(places[t], w3_q, t, codes, scales)
 
-        def bank(name, n, parts):
-            return psum.tile([P, parts, SLICE], F32, name=name, tag="bank%d" % n)
+        def h_bank(name, number, parts):
+            return psum.tile([P, parts, SLICE], F32, name=name, tag="bank%d" % number)
 
-        def leave(name, src, parts, engine, tag=None):
-            h = sb(name, [P, parts, SLICE], F32, tag)
-            evacuate(engine, h[:], src[:])
+        def h_banks(s):
+            low, high = h_bank("h_ps%d_0" % s, 2 * s, 2), h_bank("h_ps%d_1" % s, 2 * s + 1, 2)
+            return low, high, [low[:, 0, :], low[:, 1, :], high[:, 0, :], high[:, 1, :]]
+
+        def leave(name, bank, parts, copy, after=None):
+            h = sb(name, [P, parts, SLICE], F32, after)
+            copy(h[:], bank[:])
             return h
 
         def put(t, start, count, values):
-            nc.vector.tensor_copy(page[t][:].indirect(cols(slot_t, start, count)), values)
+            nc.vector.tensor_copy(page[t][:].indirect(entries(slot_t, start, count)), values)
 
-        def put_pair(s, u, src, engine, tag=None):
-            h = leave("h%d_%d" % (s, u), src, 2, engine, tag)
+        def put_pair(s, u, bank, copy, after=None):
+            h = leave("h%d_%d" % (s, u), bank, 2, copy, after)
             for e in range(2):
                 put(2 * u + e, s * SLICE, SLICE, h[:, e, :])
 
-        def pairs(s):
-            a, b = bank("h_ps%d_0" % s, 2 * s, 2), bank("h_ps%d_1" % s, 2 * s + 1, 2)
-            return a, b, [a[:, 0, :], a[:, 1, :], b[:, 0, :], b[:, 1, :]]
-
-        pg0 = sb("pg0", [P, PACK, SLICE], F32, "y_win0")
+        pg0 = look_up("pg", p, n2_t, 0, after="y_win0")
+        low0, high0, places = h_banks(0)
+        right0, left0 = sides(0)
         for t in range(PACK):
-            gather("s", pg0[:, t, :], p_t[t], cols(n2_t, 0, SLICE))
-        g0 = (pg0, qg0)
-        a0, b0, places = pairs(0)
-        layer(0, cross(0, *g0), places)
-        g1 = look_up(1, "ssss", "ssss", "y_win1", "c3_got")
-        z1 = cross(1, *g1, "z0", "y_win1")
-        put_pair(0, 0, a0, "s")
-        g2 = look_up(2, "ssss", "ssss", "y_win0", "z_codes0")
-        a1, b1, places = pairs(1)
+            g = gain[:, t : t + 1]
+            nc.vector.scalar_tensor_tensor(right0[:, t, :], q[t][:, :SLICE], g, pg0[:, t, :], ALU.mult, ALU.mult)
+            nc.vector.scalar_tensor_tensor(left0[:, t, :], p[t][:, :SLICE], g, qg0[:, t, :], ALU.mult, ALU.mult)
+        layer(0, difference(nc.vector, 0, left0, right0), places)
+
+        pg1 = look_up("pg", p, n2_t, 1, after="y_win1")
+        qg1 = look_up("qg", q, n1_t, 1, after="c3_got")
+        right1, left1 = sides(1, right_after="z0", left_after="y_win1")
+        times(nc.vector, right1, q_gain, pg1, 1)
+        times(nc.vector, left1, p_gain, qg1, 1)
+        z1 = difference(nc.gpsimd, 1, left1, right1)
+
+        put_pair(0, 0, low0, nc.vector.tensor_copy)
+        pg2 = look_up("pg", p, n2_t, 2, after="y_win0")
+        qg2 = look_up("qg", q, n1_t, 2, after="z_codes0")
+        low1, high1, places = h_banks(1)
         layer(1, z1, places)
-        put_pair(0, 1, b0, "s", "z0")
-        z2 = cross(2, *g2, "c3_got", "z1")
-        put_pair(1, 0, a1, "s")
-        g3 = look_up(3, "ssss", "ssss", "y_win1", "z_codes1")
-        a2, b2, last = bank("h_ps2_0", 4, 2), bank("h_ps2_2", 5, 1), bank("h_last", 6, 2)
-        layer(2, z2, [a2[:, 0, :], a2[:, 1, :], b2[:, 0, :], last[:, 0, :]])
-        put_pair(1, 1, b1, "s", "z1")
-        z3 = cross(3, *g3, "z_codes0", "z2")
-        put_pair(2, 0, a2, "s")
-        a3, b3 = bank("h_ps3_0", 7, 2), bank("h_ps3_2", 0, 1)
-        layer(3, z3, [a3[:, 0, :], a3[:, 1, :], b3[:, 0, :], last[:, 1, :]])
-        put(2, 2 * SLICE, SLICE, leave("h2_2", b2, 1, "s", "z2")[:, 0, :])
-        put_pair(3, 0, a3, "s")
-        put(2, 3 * SLICE, SLICE, leave("h3_2", b3, 1, "s")[:, 0, :])
-        put(3, 2 * SLICE, 2 * SLICE, leave("h_last_sb", last, 2, "s")[:].rearrange("p a b -> p (a b)"))
+        put_pair(0, 1, high0, nc.scalar.copy, after="z0")
+
+        right2, left2 = sides(2, right_after="c3_got", left_after="z1")
+        times(nc.gpsimd, right2, q_gain, pg2, 2)
+        times(nc.vector, left2, p_gain, qg2, 2)
+        z2 = difference(nc.gpsimd, 2, left2, right2)
+        put_pair(1, 0, low1, nc.scalar.copy)
+        pg3 = look_up("pg", p, n2_t, 3, after="y_win1")
+        qg3 = look_up("qg", q, n1_t, 3, after="z_codes1")
+        low2, mid2, last = h_bank("h_ps2_0", 4, 2), h_bank("h_ps2_2", 5, 1), h_bank("h_last", 6, 2)
+        layer(2, z2, [low2[:, 0, :], low2[:, 1, :], mid2[:, 0, :], last[:, 0, :]])
+        put_pair(1, 1, high1, nc.scalar.copy, after="z1")
+
+        right3, left3 = sides(3, right_after="z_codes0", left_after="z2")
+        times(nc.gpsimd, right3, q_gain, pg3, 3)
+        times(nc.gpsimd, left3, p_gain, qg3, 3)
+        z3 = difference(nc.gpsimd, 3, left3, right3)
+        put_pair(2, 0, low2, nc.scalar.copy)
+        low3, mid3 = h_bank("h_ps3_0", 7, 2), h_bank("h_ps3_2", 0, 1)
+        layer(3, z3, [low3[:, 0, :], low3[:, 1, :], mid3[:, 0, :], last[:, 1, :]])
+        put(2, 2 * SLICE, SLICE, leave("h2_2", mid2, 1, nc.scalar.copy, after="z2")[:, 0, :])
+        put_pair(3, 0, low3, nc.scalar.copy)
+        put(2, 3 * SLICE, SLICE, leave("h3_2", mid3, 1, nc.scalar.copy)[:, 0, :])
+        put(3, 2 * SLICE, 2 * SLICE, leave("h_last_sb", last, 2, nc.scalar.copy)[:].rearrange("p a b -> p (a b)"))
+
         for t in range(PACK):
             nc.sync.dma_start(out_rows[t], page[t][:])

from contextlib import ExitStack

import concourse.mybir as mybir

T, S, U = 2048, 512, 1024
WIDTH = 512
FLOPS = 3 * 2 * WIDTH * WIDTH * S

F32 = mybir.dt.float32
BF16 = mybir.dt.bfloat16
I32 = mybir.dt.int32
U32 = mybir.dt.uint32
U16 = mybir.dt.uint16
U8 = mybir.dt.uint8
FP8X4 = mybir.dt.float8_e4m3fn_x4
ALU = mybir.AluOpType
COPY = mybir.ActivationFunctionType.Copy

P = 128
PACK = 4
HALF = S // 2
SLICE = 128
REST = S - SLICE


def tile_picked_wedge2_none_p_kernel(
    tc, x_words, x_scales, w1, w2, gn, w3, mem, offs, two, n1, n2, slot, out
):
    nc = tc.nc
    with ExitStack() as ctx:
        keep = ctx.enter_context(tc.tile_pool(name="keep", bufs=1))
        psum = ctx.enter_context(tc.psum_pool(name="psum", bufs=1))

        def sb(name, shape, dtype, after=None):
            return keep.tile(shape, dtype, name=name, tag=after or name, align_bytes=64)

        def load_list(name, src):
            held = keep.tile([P, S // 16], U16, name=name)
            nc.sync.dma_start(held[:], src)
            return held

        def entries(lst, start, count):
            return lst[:, start // 16 : (start + count) // 16]

        def load_weight(name, w):
            raw = sb(name + "_raw", [P, PACK, WIDTH], F32)
            nc.sync.dma_start(raw[:], w.rearrange("(p j) c -> p j c", j=PACK))
            return raw

        def vector_gather(dst, window, offsets):
            nc.vector.tensor_copy(dst, window[:].indirect(offsets))

        def scalar_gather(dst, window, offsets):
            nc.scalar.activation(dst, window[:].indirect(offsets), COPY)

        xs = sb("xs", [P, T], U8)
        nc.vector.memset(xs[:].bitcast(I32), 0)
        xw = sb("xw", [P, T], U32)
        xw_rows = x_words[0].rearrange("p n t -> p (n t)").bitcast(I32)
        nc.sync.dma_start(xw[:, : T // 2].bitcast(I32), xw_rows[:, : T // 2])
        for r in range(4):
            nc.sync.dma_start(xs[r:P:32, :].bitcast(I32), x_scales[0, r:16:4, :].bitcast(I32))
        offs_t = load_list("offs_t", offs)
        two_t = load_list("two_t", two)
        w1_raw = load_weight("w1", w1)
        nc.sync.dma_start(xw[:, T // 2 :].bitcast(I32), xw_rows[:, T // 2 :])
        n1_t = load_list("n1_t", n1)
        w2_raw = load_weight("w2", w2)
        n2_t = load_list("n2_t", n2)
        w3_raw = load_weight("w3", w3)
        gain = sb("gain", [P, PACK], F32)
        nc.sync.dma_start(gain[:], gn.rearrange("(p t) o -> p (t o)", t=PACK))
        slot_t = load_list("slot_t", slot)
        mem_rows = mem.rearrange("(p t) u -> t p u", t=PACK)
        out_rows = out.rearrange("(p t) u -> t p u", t=PACK)
        page = []
        for t in range(PACK):
            page.append(sb("page%d" % t, [P, U], F32))
            nc.sync.dma_start(page[t][:], mem_rows[t])

        def round_halves(name, raw, copy):
            halves = []
            for u in range(2):
                half = sb("%s_bf%d" % (name, u), [P, 2 * P * PACK], BF16)
                src = raw[:].rearrange("p j (m u t) -> p u m j t", u=2, t=2)[:, u]
                copy(half[:].rearrange("p (t m j) -> p m j t", t=2, j=PACK), src)
                halves.append(half)
            return halves

        def quantize(name, values, words):
            codes = sb(name % "codes", [P, words], U32)
            scales = sb(name % "scales", [P, words], U8)
            nc.vector.quantize_mx(out=codes[:].bitcast(FP8X4), scales=scales[:], in_=values[:])
            return codes, scales

        def product(dst, weight_halves, t, codes, scales):
            w_codes, w_scales = weight_halves[t // 2]
            m = slice((t % 2) * P, (t % 2 + 1) * P)
            nc.tensor.matmul_mx(
                out=dst, lhsT=w_codes[:, m].bitcast(FP8X4), lhsT_scale=w_scales[:, m],
                rhs=codes[:].bitcast(FP8X4), rhs_scale=scales[:], start=True, stop=True,
            )

        def projection(name, first_bank, weight_halves, codes, scales):
            banks = []
            for t in range(PACK):
                banks.append(psum.tile([P, S], F32, name="%s_ps%d" % (name, t), tag="bank%d" % (first_bank + t)))
                product(banks[t][:], weight_halves, t, codes, scales)
            return banks

        s1 = sb("s1", [P, S], U8)
        vector_gather(s1[:], xs, offs_t[:])
        s2 = sb("s2", [P, S], U8)
        vector_gather(s2[:], xs, two_t[:])
        w1_bf = round_halves("w1", w1_raw, nc.scalar.copy)
        w1_q = [quantize("w1_%s0", w1_bf[0], 2 * P)]
        x1 = sb("x1", [P, S], U32)
        vector_gather(x1[:], xw, offs_t[:])
        w1_q.append(quantize("w1b_%s0", w1_bf[1], 2 * P))
        y_ps = projection("y", 0, w1_q, x1, s1)
        x2 = sb("x2", [P, S], U32, after="w1_bf0")
        vector_gather(x2[:], xw, two_t[:])
        w2_bf = round_halves("w2", w2_raw, nc.vector.tensor_copy)
        w2_q = [quantize("w2_%%s%d" % u, w2_bf[u], 2 * P) for u in range(2)]
        c_ps = projection("c", PACK, w2_q, x2, s2)

        def window(name, bank, copy, after=None):
            win = sb(name + "_win", [P, S], F32, after)
            copy(win[:], bank[:])
            return win

        def fetch(name, win, lst, gather):
            got = sb(name + "_got", [P, S], F32)
            for start in range(0, S, HALF):
                gather(got[:, start : start + HALF], win, entries(lst, start, HALF))
            return got

        def extreme(name, bank, got, op, after=None):
            res = sb(name, [P, S], F32, after)
            nc.vector.tensor_tensor(res[:], bank[:], got[:], op)
            return res

        p_gain = sb("p_gain", [P, PACK, REST], F32)
        q_gain = sb("q_gain", [P, PACK, REST], F32)

        p, q = [None] * PACK, [None] * PACK
        y_got = []
        for t in range(PACK):
            y_win = window("y%d" % t, y_ps[t], nc.scalar.copy, after="y_win%d" % (t % 2))
            y_got.append(fetch("y%d" % t, y_win, n1_t, scalar_gather))
        c0_win = window("c0", c_ps[0], nc.vector.tensor_copy)
        c1_win = window("c1", c_ps[1], nc.vector.tensor_copy)
        p[0] = extreme("p0", y_ps[0], y_got[0], ALU.max, after="w2_bf0")
        q[0] = extreme("q0", c_ps[0], fetch("c0", c0_win, n2_t, vector_gather), ALU.min)
        p[1] = extreme("p1", y_ps[1], y_got[1], ALU.max, after="c0_win")
        q[1] = extreme("q1", c_ps[1], fetch("c1", c1_win, n2_t, vector_gather), ALU.min)
        p[2] = extreme("p2", y_ps[2], y_got[2], ALU.max, after="c1_win")
        p[3] = extreme("p3", y_ps[3], y_got[3], ALU.max, after="c1_got")

        w3_bf = sb("w3_bf", [P, PACK * P * PACK], BF16, after="w2_bf1")
        nc.gpsimd.tensor_scalar(
            w3_bf[:].rearrange("p (t m j) -> p m t j", t=PACK, j=PACK),
            w3_raw[:].rearrange("p j (m t) -> p m t j", t=PACK), 1.0, 0.0, ALU.mult, ALU.add,
        )
        w3_codes, w3_scales = quantize("w3_%s", w3_bf, PACK * P)
        w3_q = [(w3_codes[:, : 2 * P], w3_scales[:, : 2 * P]), (w3_codes[:, 2 * P :], w3_scales[:, 2 * P :])]

        c2_win = window("c2", c_ps[2], nc.scalar.copy, after="y_win0")
        q[2] = extreme("q2", c_ps[2], fetch("c2", c2_win, n2_t, scalar_gather), ALU.min, after="w2_bf1")
        c3_win = window("c3", c_ps[3], nc.scalar.copy, after="y_win1")
        c3_got = fetch("c3", c3_win, n2_t, scalar_gather)
        qg0 = sb("qg0", [P, PACK, SLICE], F32)
        for t in range(PACK - 1):
            vector_gather(qg0[:, t, :], q[t], entries(n1_t, 0, SLICE))
        q[3] = extreme("q3", c_ps[3], c3_got, ALU.min, after="c2_got")
        vector_gather(qg0[:, 3, :], q[3], entries(n1_t, 0, SLICE))
        for t in range(PACK):
            for dst, src in ((p_gain, p[t]), (q_gain, q[t])):
                nc.gpsimd.tensor_scalar(dst[:, t, :], src[:, SLICE:], gain[:, t : t + 1], 0.0, ALU.mult, ALU.add)

        def look_up(name, tiles, lst, s, after):
            got = sb("%s%d" % (name, s), [P, PACK, SLICE], F32, after)
            for t in range(PACK):
                scalar_gather(got[:, t, :], tiles[t], entries(lst, s * SLICE, SLICE))
            return got

        def sides(s, right_after=None, left_after=None):
            right = sb("right%d" % s, [P, PACK, SLICE], F32, right_after)
            left = sb("left%d" % s, [P, PACK, SLICE], F32, left_after)
            return right, left

        def times(engine, dst, scaled, got, s):
            engine.tensor_tensor(dst[:], scaled[:, :, (s - 1) * SLICE : s * SLICE], got[:], ALU.mult)

        def difference(engine, s, left, right):
            z = sb("z%d" % s, [P, SLICE * PACK], BF16)
            walk = "p t (c i) -> p c t i"
            engine.tensor_tensor(
                z[:].rearrange("p (c i t) -> p c t i", i=2, t=PACK),
                left[:].rearrange(walk, i=2), right[:].rearrange(walk, i=2), ALU.subtract,
            )
            return z

        def layer(s, z, places):
            codes, scales = quantize("z_%%s%d" % s, z, SLICE)
            for t in range(PACK):
                product(places[t], w3_q, t, codes, scales)

        def h_bank(name, number, parts):
            return psum.tile([P, parts, SLICE], F32, name=name, tag="bank%d" % number)

        def h_banks(s):
            low, high = h_bank("h_ps%d_0" % s, 2 * s, 2), h_bank("h_ps%d_1" % s, 2 * s + 1, 2)
            return low, high, [low[:, 0, :], low[:, 1, :], high[:, 0, :], high[:, 1, :]]

        def leave(name, bank, parts, copy, after=None):
            h = sb(name, [P, parts, SLICE], F32, after)
            copy(h[:], bank[:])
            return h

        def put(t, start, count, values):
            nc.vector.tensor_copy(page[t][:].indirect(entries(slot_t, start, count)), values)

        def put_pair(s, u, bank, copy, after=None):
            h = leave("h%d_%d" % (s, u), bank, 2, copy, after)
            for e in range(2):
                put(2 * u + e, s * SLICE, SLICE, h[:, e, :])

        pg0 = look_up("pg", p, n2_t, 0, after="y_win0")
        low0, high0, places = h_banks(0)
        right0, left0 = sides(0)
        for t in range(PACK):
            g = gain[:, t : t + 1]
            nc.vector.scalar_tensor_tensor(right0[:, t, :], q[t][:, :SLICE], g, pg0[:, t, :], ALU.mult, ALU.mult)
            nc.vector.scalar_tensor_tensor(left0[:, t, :], p[t][:, :SLICE], g, qg0[:, t, :], ALU.mult, ALU.mult)
        layer(0, difference(nc.vector, 0, left0, right0), places)

        pg1 = look_up("pg", p, n2_t, 1, after="y_win1")
        qg1 = look_up("qg", q, n1_t, 1, after="c3_got")
        right1, left1 = sides(1, right_after="z0", left_after="y_win1")
        times(nc.vector, right1, q_gain, pg1, 1)
        times(nc.vector, left1, p_gain, qg1, 1)
        z1 = difference(nc.gpsimd, 1, left1, right1)

        put_pair(0, 0, low0, nc.vector.tensor_copy)
        pg2 = look_up("pg", p, n2_t, 2, after="y_win0")
        qg2 = look_up("qg", q, n1_t, 2, after="z_codes0")
        low1, high1, places = h_banks(1)
        layer(1, z1, places)
        put_pair(0, 1, high0, nc.scalar.copy, after="z0")

        right2, left2 = sides(2, right_after="c3_got", left_after="z1")
        times(nc.gpsimd, right2, q_gain, pg2, 2)
        times(nc.vector, left2, p_gain, qg2, 2)
        z2 = difference(nc.gpsimd, 2, left2, right2)
        put_pair(1, 0, low1, nc.scalar.copy)
        pg3 = look_up("pg", p, n2_t, 3, after="y_win1")
        qg3 = look_up("qg", q, n1_t, 3, after="z_codes1")
        low2, mid2, last = h_bank("h_ps2_0", 4, 2), h_bank("h_ps2_2", 5, 1), h_bank("h_last", 6, 2)
        layer(2, z2, [low2[:, 0, :], low2[:, 1, :], mid2[:, 0, :], last[:, 0, :]])
        put_pair(1, 1, high1, nc.scalar.copy, after="z1")

        right3, left3 = sides(3, right_after="z_codes0", left_after="z2")
        times(nc.gpsimd, right3, q_gain, pg3, 3)
        times(nc.gpsimd, left3, p_gain, qg3, 3)
        z3 = difference(nc.gpsimd, 3, left3, right3)
        put_pair(2, 0, low2, nc.scalar.copy)
        low3, mid3 = h_bank("h_ps3_0", 7, 2), h_bank("h_ps3_2", 0, 1)
        layer(3, z3, [low3[:, 0, :], low3[:, 1, :], mid3[:, 0, :], last[:, 1, :]])
        put(2, 2 * SLICE, SLICE, leave("h2_2", mid2, 1, nc.scalar.copy, after="z2")[:, 0, :])
        put_pair(3, 0, low3, nc.scalar.copy)
        put(2, 3 * SLICE, SLICE, leave("h3_2", mid3, 1, nc.scalar.copy)[:, 0, :])
        put(3, 2 * SLICE, 2 * SLICE, leave("h_last_sb", last, 2, nc.scalar.copy)[:].rearrange("p a b -> p (a b)"))

        for t in range(PACK):
            nc.sync.dma_start(out_rows[t], page[t][:])
